import numpy as np
import ml_dtypes

BF16 = ml_dtypes.bfloat16


def bf(x):
    return np.asarray(x, np.float32).astype(BF16)


def f32(x):
    return np.asarray(x, np.float32)


def f64(x):
    return np.asarray(x).astype(np.float64)


def striped(idx):
    return np.tile(idx.reshape(-1, 16).T, (8, 1))


S, K, M, N = 512, 128, 256, 256


def setup_inputs():
    return {"base": bf(np.random.standard_normal((M, S))), "x": bf(np.random.standard_normal((K, N))), "w": bf(np.random.standard_normal((K, M)) / np.sqrt(K)), "b": f32(0.5 * np.random.standard_normal((M, 1))), "offs": striped(np.random.permutation(S)[:N])}


def reference(base, x, w, b, offs):
    idx = offs[:16].T.reshape(-1)
    z = f64(base).copy()
    z[:, idx] = f64(w).T @ f64(x)
    return np.maximum(z + f64(b), 0.0)

@@ -1,0 +1,58 @@
+import concourse.mybir as mybir
+from concourse.masks import make_identity
+
+P = 128
+S = 512
+K = 128
+M = 256
+N = 256
+BLOCKS = M // P
+
+FLOPS = 2 * K * M * N
+
+BF16, F32, U16 = mybir.dt.bfloat16, mybir.dt.float32, mybir.dt.uint16
+RELU = mybir.ActivationFunctionType.Relu
+ADD, MAX = mybir.AluOpType.add, mybir.AluOpType.max
+
+
+def tile_scatter_matmul_kernel(tc, base, x, w, b, offs, out):
+    nc = tc.nc
+    with (
+        tc.tile_pool(name="held", bufs=1) as held,
+        tc.psum_pool(name="psum", bufs=1) as psum,
+    ):
+        offsets = held.tile([P, N // 16], U16, name="offsets")
+        nc.sync.dma_start(offsets[:], offs)
+
+        base_tiles = [held.tile([P, S], BF16, name=f"base{a}") for a in range(BLOCKS)]
+        nc.sync.dma_start(base_tiles[0][:], base[0:P, :])
+        nc.scalar.dma_start(base_tiles[1][:], base[P : 2 * P, :])
+        x_tile = held.tile([K, N], BF16, name="x_tile")
+        nc.sync.dma_start(x_tile[:], x)
+        w_tile = held.tile([K, M], BF16, name="w_tile")
+        nc.scalar.dma_start(w_tile[:], w)
+        bias = held.tile([P, BLOCKS], F32, name="bias")
+        nc.scalar.dma_start(bias[:], b.rearrange("(a p) o -> p (a o)", p=P))
+
+        ident = held.tile([P, P], BF16, name="ident")
+        make_identity(nc, ident[:])
+
+        windows = [psum.tile([P, S], F32, name=f"window{a}") for a in range(BLOCKS)]
+        for a in range(BLOCKS):
+            nc.tensor.matmul(windows[a][:], ident[:], base_tiles[a][:], start=True, stop=True)
+
+        for a in range(BLOCKS):
+            nc.tensor.matmul(
+                windows[a][:].indirect(offsets[:]),
+                w_tile[:, a * P : (a + 1) * P],
+                x_tile[:],
+                start=True,
+                stop=True,
+            )
+
+        result0 = held.tile([P, S], F32, name="result0")
+        nc.scalar.activation(result0[:], windows[0][:], RELU, bias=bias[:, 0:1])
+        nc.sync.dma_start(out[0:P, :], result0[:])
+        result1 = held.tile([P, S], F32, name="result1")
+        nc.vector.tensor_scalar(result1[:], windows[1][:], bias[:, 1:2], 0.0, ADD, MAX)
+        nc.scalar.dma_start(out[P : 2 * P, :], result1[:])

@@ -21,18 +21,21 @@ def tile_scatter_matmul_kernel(tc, base, x, w, b, offs, out):
         tc.tile_pool(name="held", bufs=1) as held,
         tc.psum_pool(name="psum", bufs=1) as psum,
     ):
-        offsets = held.tile([P, N // 16], U16, name="offsets")
-        nc.sync.dma_start(offsets[:], offs)
-
         base_tiles = [held.tile([P, S], BF16, name=f"base{a}") for a in range(BLOCKS)]
         nc.sync.dma_start(base_tiles[0][:], base[0:P, :])
         nc.scalar.dma_start(base_tiles[1][:], base[P : 2 * P, :])
-        x_tile = held.tile([K, N], BF16, name="x_tile")
-        nc.sync.dma_start(x_tile[:], x)
+        offsets = held.tile([P, N // 16], U16, name="offsets")
+        nc.sync.dma_start(offsets[:], offs)
         w_tile = held.tile([K, M], BF16, name="w_tile")
         nc.scalar.dma_start(w_tile[:], w)
+        x_tile = held.tile([K, N], BF16, name="x_tile")
+        nc.sync.dma_start(x_tile[:], x)
         bias = held.tile([P, BLOCKS], F32, name="bias")
         nc.scalar.dma_start(bias[:], b.rearrange("(a p) o -> p (a o)", p=P))
+
+        scratch = held.tile([P, 1], F32, name="scratch")
+        nc.vector.memset(scratch[:], 0.0)
+        nc.scalar.activation(scratch[:], scratch[:], RELU)
 
         ident = held.tile([P, P], BF16, name="ident")
         make_identity(nc, ident[:])
@@ -51,8 +54,8 @@ def tile_scatter_matmul_kernel(tc, base, x, w, b, offs, out):
             )
 
         result0 = held.tile([P, S], F32, name="result0")
-        nc.scalar.activation(result0[:], windows[0][:], RELU, bias=bias[:, 0:1])
+        nc.vector.tensor_scalar(result0[:], windows[0][:], bias[:, 0:1], 0.0, ADD, MAX)
         nc.sync.dma_start(out[0:P, :], result0[:])
         result1 = held.tile([P, S], F32, name="result1")
-        nc.vector.tensor_scalar(result1[:], windows[1][:], bias[:, 1:2], 0.0, ADD, MAX)
+        nc.scalar.activation(result1[:], windows[1][:], RELU, bias=bias[:, 1:2])
         nc.scalar.dma_start(out[P : 2 * P, :], result1[:])

@@ -8,6 +8,8 @@ M = 256
 N = 256
 BLOCKS = M // P
 
+WARM_UP = 3
+
 FLOPS = 2 * K * M * N
 
 BF16, F32, U16 = mybir.dt.bfloat16, mybir.dt.float32, mybir.dt.uint16
@@ -32,6 +34,12 @@ def tile_scatter_matmul_kernel(tc, base, x, w, b, offs, out):
         nc.sync.dma_start(x_tile[:], x)
         bias = held.tile([P, BLOCKS], F32, name="bias")
         nc.scalar.dma_start(bias[:], b.rearrange("(a p) o -> p (a o)", p=P))
+
+        zeros = held.tile([P, S], BF16, name="zeros")
+        nc.vector.memset(zeros[:], 0.0)
+        idle_bank = psum.tile([P, S], F32, name="idle_bank")
+        for _ in range(WARM_UP):
+            nc.tensor.matmul(idle_bank[:], zeros[:, 0:P], zeros[:], start=True, stop=True)
 
         scratch = held.tile([P, 1], F32, name="scratch")
         nc.vector.memset(scratch[:], 0.0)

@@ -8,6 +8,9 @@ M = 256
 N = 256
 BLOCKS = M // P
 
+HALVES = 2
+HALF = S // HALVES
+
 WARM_UP = 3
 
 FLOPS = 2 * K * M * N
@@ -61,9 +64,14 @@ def tile_scatter_matmul_kernel(tc, base, x, w, b, offs, out):
                 stop=True,
             )
 
-        result0 = held.tile([P, S], F32, name="result0")
-        nc.vector.tensor_scalar(result0[:], windows[0][:], bias[:, 0:1], 0.0, ADD, MAX)
-        nc.sync.dma_start(out[0:P, :], result0[:])
-        result1 = held.tile([P, S], F32, name="result1")
-        nc.scalar.activation(result1[:], windows[1][:], RELU, bias=bias[:, 1:2])
-        nc.scalar.dma_start(out[P : 2 * P, :], result1[:])
+        for h in range(HALVES):
+            cols = slice(h * HALF, (h + 1) * HALF)
+            result0 = held.tile([P, HALF], F32, name=f"result0_{h}")
+            nc.vector.tensor_scalar(result0[:], windows[0][:, cols], bias[:, 0:1], 0.0, ADD, MAX)
+            nc.sync.dma_start(out[0:P, cols], result0[:])
+        for h in range(HALVES):
+            cols = slice(h * HALF, (h + 1) * HALF)
+            result1 = held.tile([P, HALF], F32, name=f"result1_{h}")
+            nc.scalar.activation(result1[:], windows[1][:, cols], RELU, bias=bias[:, 1:2])
+            queue = nc.scalar if h == HALVES - 1 else nc.sync
+            queue.dma_start(out[P : 2 * P, cols], result1[:])

@@ -7,6 +7,7 @@ K = 128
 M = 256
 N = 256
 BLOCKS = M // P
+SQUARE = 32
 
 HALVES = 2
 HALF = S // HALVES
@@ -27,16 +28,14 @@ def tile_scatter_matmul_kernel(tc, base, x, w, b, offs, out):
         tc.psum_pool(name="psum", bufs=1) as psum,
     ):
         base_tiles = [held.tile([P, S], BF16, name=f"base{a}") for a in range(BLOCKS)]
-        nc.sync.dma_start(base_tiles[0][:], base[0:P, :])
-        nc.scalar.dma_start(base_tiles[1][:], base[P : 2 * P, :])
+        for a in range(BLOCKS):
+            nc.sync.dma_start(base_tiles[a][:], base[a * P : (a + 1) * P, :])
         offsets = held.tile([P, N // 16], U16, name="offsets")
         nc.sync.dma_start(offsets[:], offs)
         w_tile = held.tile([K, M], BF16, name="w_tile")
-        nc.scalar.dma_start(w_tile[:], w)
+        nc.sync.dma_start(w_tile[:], w)
         x_tile = held.tile([K, N], BF16, name="x_tile")
         nc.sync.dma_start(x_tile[:], x)
-        bias = held.tile([P, BLOCKS], F32, name="bias")
-        nc.scalar.dma_start(bias[:], b.rearrange("(a p) o -> p (a o)", p=P))
 
         zeros = held.tile([P, S], BF16, name="zeros")
         nc.vector.memset(zeros[:], 0.0)
@@ -44,8 +43,19 @@ def tile_scatter_matmul_kernel(tc, base, x, w, b, offs, out):
         for _ in range(WARM_UP):
             nc.tensor.matmul(idle_bank[:], zeros[:, 0:P], zeros[:], start=True, stop=True)
 
+        bias_rows = held.tile([P, BLOCKS * SQUARE], F32, name="bias_rows", align_bytes=64)
+        nc.vector.memset(bias_rows[:], 0.0)
+        nc.scalar.dma_start(
+            bias_rows[0:P:SQUARE, :].rearrange("q (a r) -> q a r", a=BLOCKS),
+            b.rearrange("(a q r) o -> q a (r o)", a=BLOCKS, r=SQUARE),
+        )
+        bias = held.tile([P, BLOCKS * SQUARE], F32, name="bias", align_bytes=64)
+        for a in range(BLOCKS):
+            square = slice(a * SQUARE, (a + 1) * SQUARE)
+            nc.vector.transpose(bias[:, square], bias_rows[:, square])
+
         scratch = held.tile([P, 1], F32, name="scratch")
-        nc.vector.memset(scratch[:], 0.0)
+        nc.gpsimd.memset(scratch[:], 0.0)
         nc.scalar.activation(scratch[:], scratch[:], RELU)
 
         ident = held.tile([P, P], BF16, name="ident")
@@ -72,6 +82,6 @@ def tile_scatter_matmul_kernel(tc, base, x, w, b, offs, out):
         for h in range(HALVES):
             cols = slice(h * HALF, (h + 1) * HALF)
             result1 = held.tile([P, HALF], F32, name=f"result1_{h}")
-            nc.scalar.activation(result1[:], windows[1][:, cols], RELU, bias=bias[:, 1:2])
+            nc.scalar.activation(result1[:], windows[1][:, cols], RELU, bias=bias[:, SQUARE : SQUARE + 1])
             queue = nc.scalar if h == HALVES - 1 else nc.sync
             queue.dma_start(out[P : 2 * P, cols], result1[:])

@@ -28,14 +28,11 @@ def tile_scatter_matmul_kernel(tc, base, x, w, b, offs, out):
         tc.psum_pool(name="psum", bufs=1) as psum,
     ):
         base_tiles = [held.tile([P, S], BF16, name=f"base{a}") for a in range(BLOCKS)]
-        for a in range(BLOCKS):
-            nc.sync.dma_start(base_tiles[a][:], base[a * P : (a + 1) * P, :])
+        nc.sync.dma_start(base_tiles[0][:], base[0:P, :])
         offsets = held.tile([P, N // 16], U16, name="offsets")
         nc.sync.dma_start(offsets[:], offs)
         w_tile = held.tile([K, M], BF16, name="w_tile")
         nc.sync.dma_start(w_tile[:], w)
-        x_tile = held.tile([K, N], BF16, name="x_tile")
-        nc.sync.dma_start(x_tile[:], x)
 
         zeros = held.tile([P, S], BF16, name="zeros")
         nc.vector.memset(zeros[:], 0.0)
@@ -49,6 +46,10 @@ def tile_scatter_matmul_kernel(tc, base, x, w, b, offs, out):
             bias_rows[0:P:SQUARE, :].rearrange("q (a r) -> q a r", a=BLOCKS),
             b.rearrange("(a q r) o -> q a (r o)", a=BLOCKS, r=SQUARE),
         )
+        nc.scalar.dma_start(base_tiles[1][:], base[P : 2 * P, :])
+        x_tile = held.tile([K, N], BF16, name="x_tile")
+        nc.scalar.dma_start(x_tile[:], x)
+
         bias = held.tile([P, BLOCKS * SQUARE], F32, name="bias", align_bytes=64)
         for a in range(BLOCKS):
             square = slice(a * SQUARE, (a + 1) * SQUARE)

@@ -33,6 +33,9 @@ def tile_scatter_matmul_kernel(tc, base, x, w, b, offs, out):
         nc.sync.dma_start(offsets[:], offs)
         w_tile = held.tile([K, M], BF16, name="w_tile")
         nc.sync.dma_start(w_tile[:], w)
+        nc.scalar.dma_start(base_tiles[1][:], base[P : 2 * P, :])
+        x_tile = held.tile([K, N], BF16, name="x_tile")
+        nc.scalar.dma_start(x_tile[:], x)
 
         zeros = held.tile([P, S], BF16, name="zeros")
         nc.vector.memset(zeros[:], 0.0)
@@ -46,10 +49,6 @@ def tile_scatter_matmul_kernel(tc, base, x, w, b, offs, out):
             bias_rows[0:P:SQUARE, :].rearrange("q (a r) -> q a r", a=BLOCKS),
             b.rearrange("(a q r) o -> q a (r o)", a=BLOCKS, r=SQUARE),
         )
-        nc.scalar.dma_start(base_tiles[1][:], base[P : 2 * P, :])
-        x_tile = held.tile([K, N], BF16, name="x_tile")
-        nc.scalar.dma_start(x_tile[:], x)
-
         bias = held.tile([P, BLOCKS * SQUARE], F32, name="bias", align_bytes=64)
         for a in range(BLOCKS):
             square = slice(a * SQUARE, (a + 1) * SQUARE)

@@ -12,7 +12,7 @@ SQUARE = 32
 HALVES = 2
 HALF = S // HALVES
 
-WARM_UP = 3
+WARM_UP = 3 * S // P
 
 FLOPS = 2 * K * M * N
 
@@ -37,11 +37,11 @@ def tile_scatter_matmul_kernel(tc, base, x, w, b, offs, out):
         x_tile = held.tile([K, N], BF16, name="x_tile")
         nc.scalar.dma_start(x_tile[:], x)
 
-        zeros = held.tile([P, S], BF16, name="zeros")
+        zeros = held.tile([P, P], BF16, name="zeros")
         nc.vector.memset(zeros[:], 0.0)
-        idle_bank = psum.tile([P, S], F32, name="idle_bank")
+        idle_bank = psum.tile([P, P], F32, name="idle_bank")
         for _ in range(WARM_UP):
-            nc.tensor.matmul(idle_bank[:], zeros[:, 0:P], zeros[:], start=True, stop=True)
+            nc.tensor.matmul(idle_bank[:], zeros[:], zeros[:], start=True, stop=True)
 
         bias_rows = held.tile([P, BLOCKS * SQUARE], F32, name="bias_rows", align_bytes=64)
         nc.vector.memset(bias_rows[:], 0.0)

import concourse.mybir as mybir
from concourse.masks import make_identity

P = 128
S = 512
K = 128
M = 256
N = 256
BLOCKS = M // P
SQUARE = 32

HALVES = 2
HALF = S // HALVES

WARM_UP = 3 * S // P

FLOPS = 2 * K * M * N

BF16, F32, U16 = mybir.dt.bfloat16, mybir.dt.float32, mybir.dt.uint16
RELU = mybir.ActivationFunctionType.Relu
ADD, MAX = mybir.AluOpType.add, mybir.AluOpType.max


def tile_scatter_matmul_kernel(tc, base, x, w, b, offs, out):
    nc = tc.nc
    with (
        tc.tile_pool(name="held", bufs=1) as held,
        tc.psum_pool(name="psum", bufs=1) as psum,
    ):
        base_tiles = [held.tile([P, S], BF16, name=f"base{a}") for a in range(BLOCKS)]
        nc.sync.dma_start(base_tiles[0][:], base[0:P, :])
        offsets = held.tile([P, N // 16], U16, name="offsets")
        nc.sync.dma_start(offsets[:], offs)
        w_tile = held.tile([K, M], BF16, name="w_tile")
        nc.sync.dma_start(w_tile[:], w)
        nc.scalar.dma_start(base_tiles[1][:], base[P : 2 * P, :])
        x_tile = held.tile([K, N], BF16, name="x_tile")
        nc.scalar.dma_start(x_tile[:], x)

        zeros = held.tile([P, P], BF16, name="zeros")
        nc.vector.memset(zeros[:], 0.0)
        idle_bank = psum.tile([P, P], F32, name="idle_bank")
        for _ in range(WARM_UP):
            nc.tensor.matmul(idle_bank[:], zeros[:], zeros[:], start=True, stop=True)

        bias_rows = held.tile([P, BLOCKS * SQUARE], F32, name="bias_rows", align_bytes=64)
        nc.vector.memset(bias_rows[:], 0.0)
        nc.scalar.dma_start(
            bias_rows[0:P:SQUARE, :].rearrange("q (a r) -> q a r", a=BLOCKS),
            b.rearrange("(a q r) o -> q a (r o)", a=BLOCKS, r=SQUARE),
        )
        bias = held.tile([P, BLOCKS * SQUARE], F32, name="bias", align_bytes=64)
        for a in range(BLOCKS):
            square = slice(a * SQUARE, (a + 1) * SQUARE)
            nc.vector.transpose(bias[:, square], bias_rows[:, square])

        scratch = held.tile([P, 1], F32, name="scratch")
        nc.gpsimd.memset(scratch[:], 0.0)
        nc.scalar.activation(scratch[:], scratch[:], RELU)

        ident = held.tile([P, P], BF16, name="ident")
        make_identity(nc, ident[:])

        windows = [psum.tile([P, S], F32, name=f"window{a}") for a in range(BLOCKS)]
        for a in range(BLOCKS):
            nc.tensor.matmul(windows[a][:], ident[:], base_tiles[a][:], start=True, stop=True)

        for a in range(BLOCKS):
            nc.tensor.matmul(
                windows[a][:].indirect(offsets[:]),
                w_tile[:, a * P : (a + 1) * P],
                x_tile[:],
                start=True,
                stop=True,
            )

        for h in range(HALVES):
            cols = slice(h * HALF, (h + 1) * HALF)
            result0 = held.tile([P, HALF], F32, name=f"result0_{h}")
            nc.vector.tensor_scalar(result0[:], windows[0][:, cols], bias[:, 0:1], 0.0, ADD, MAX)
            nc.sync.dma_start(out[0:P, cols], result0[:])
        for h in range(HALVES):
            cols = slice(h * HALF, (h + 1) * HALF)
            result1 = held.tile([P, HALF], F32, name=f"result1_{h}")
            nc.scalar.activation(result1[:], windows[1][:, cols], RELU, bias=bias[:, SQUARE : SQUARE + 1])
            queue = nc.scalar if h == HALVES - 1 else nc.sync
            queue.dma_start(out[P : 2 * P, cols], result1[:])
